import numpy as np
import ml_dtypes


def mxq(x, axis, fmt="e4m3"):
    dtype, down = {"e4m3": (ml_dtypes.float8_e4m3fn, 7), "e5m2": (ml_dtypes.float8_e5m2, 14)}[fmt]
    v = np.moveaxis(np.asarray(x, np.float32).astype(ml_dtypes.bfloat16).astype(np.float64), axis, -1)
    blocks = v.reshape(v.shape[:-1] + (-1, 32))
    amax = np.abs(blocks).max(-1, keepdims=True)
    byte = np.maximum(np.where(amax > 0, np.frexp(amax)[1] - 1 + 127, 0) - down, 1)
    scale = np.exp2(byte - 127.0)
    codes = (blocks / scale).astype(np.float32).astype(dtype).astype(np.float64)
    return np.moveaxis((codes * scale).reshape(v.shape), -1, axis)


WIDE = False


def mx_kscale(k):
    if not WIDE:
        return np.ones(k)
    levels = np.array([10, -10, 5, -5, 0])
    if k % 512:
        return np.exp2(np.random.permutation(np.resize(levels, k // 32))).repeat(32)
    a = np.empty((k // 512, 16))
    for p in range(k // 512):
        a[p, :8] = np.random.permutation(np.resize(levels, 8))
        for g in range(8):
            far = levels[np.abs(levels - a[p, g]) >= 10]
            a[p, g + 8] = far[np.random.randint(len(far))]
    return np.exp2(a.ravel()).repeat(32)


def f64(x):
    return np.asarray(x).astype(np.float64)


def striped(idx):
    return np.tile(idx.reshape(-1, 16).T, (8, 1)).astype(np.uint16)


def unstriped(offs):
    return offs[:16].T.reshape(-1).astype(np.int64)


def striped8(idx):
    return np.concatenate([x.reshape(-1, 16).T for x in idx]).astype(np.uint16)


def runs(offs, k):
    lists = np.stack([offs[16 * r : 16 * r + 16].T.reshape(-1) for r in range(8)]).astype(np.int64)
    return lists[np.arange(k) % 512 // 64]


def pack_weight(w):
    k, n = w.shape
    w = f64(np.asarray(w, np.float32).astype(ml_dtypes.bfloat16)).reshape(k // 32, 32, n)
    amax = np.abs(w).max(1)
    byte = np.clip(np.where(amax > 0, np.frexp(amax)[1] - 1 + 127 - 7, 1), 1, 254)
    scaled = (w * np.exp2(127.0 - byte)[:, None, :]).reshape(k, n).astype(np.float32)
    words = np.ascontiguousarray(scaled.reshape(k // 512, 128, 4, n).transpose(0, 1, 3, 2)).astype(ml_dtypes.float8_e4m3fn).view(np.uint8)
    return words, np.ascontiguousarray(byte.astype(np.uint8).reshape(k // 512, 16, n))


def unpack_weight(words, scales):
    g, p, n, _ = words.shape
    vals = np.ascontiguousarray(words).view(ml_dtypes.float8_e4m3fn).astype(np.float64) * np.repeat(np.exp2(scales.astype(np.float64) - 127.0), 8, axis=1)[..., None]
    return vals.transpose(0, 1, 3, 2).reshape(g * 512, n)


K, T, S, N, H, W, J = 512, 2048, 512, 512, 512, 256, 512


def setup_inputs():
    n = np.random.standard_normal
    s = mx_kscale(K)[:, None]
    u = mx_kscale(S)
    packed_xT = pack_weight(n((K, T)) * s)
    perm = np.stack([np.random.permutation(H) for _ in range(8)])
    return {
        "x_words": packed_xT[0],
        "x_scales": packed_xT[1],
        "wa": (n((K, H)) / np.sqrt(K) / s).astype(np.float32),
        "gt": (np.random.uniform(0.5, 1.5, (S, 1)) * u[:, None]).astype(np.float32),
        "w1": (n((S, N)) / np.sqrt(S) / u[:, None]).astype(np.float32),
        "tab": np.random.uniform(0.4, 1.4, (N, J)).astype(np.float32),
        "offs": striped(np.random.permutation(T)[:S]),
        "n1": striped8(perm[:, :W]),
        "n2": striped8(perm[:, W:]),
        "n3": striped8(np.random.randint(0, J, (8, H))),
        "n4": striped8(np.stack([np.random.permutation(H) for _ in range(8)])),
    }


def reference(x_words, x_scales, wa, gt, w1, tab, offs, n1, n2, n3, n4):
    xq = unpack_weight(x_words, x_scales)[:, unstriped(offs)]
    y = xq.T @ mxq(f64(wa), 0, "e4m3")
    pa = y[np.arange(S)[:, None], runs(n1, S)]
    pb = y[np.arange(S)[:, None], runs(n2, S)]
    ra = np.maximum(pa, pb)
    ds = y.copy()
    ds[np.arange(S)[:, None], runs(n1, S)] = ra
    z = f64(gt) * ds
    h = mxq(f64(w1), 0, "e4m3").T @ mxq(z, 0, "e4m3")
    return h * (f64(tab)[np.arange(N)[:, None], runs(n3, N)]) - (0.5 * (h[np.arange(N)[:, None], runs(n4, N)]))

@@ -1,0 +1,176 @@
+from contextlib import ExitStack
+
+import concourse.mybir as mybir
+
+K, T, S, N, H, W, J = 512, 2048, 512, 512, 512, 256, 512
+FLOPS = 2 * K * S * H + 2 * S * N * H
+
+F32 = mybir.dt.float32
+BF16 = mybir.dt.bfloat16
+I32 = mybir.dt.int32
+U32 = mybir.dt.uint32
+U16 = mybir.dt.uint16
+U8 = mybir.dt.uint8
+FP8X4 = mybir.dt.float8_e4m3fn_x4
+ALU = mybir.AluOpType
+COPY = mybir.ActivationFunctionType.Copy
+
+P = 128
+PACK = 4
+HALF = H // 2
+
+
+def tile_picked_tokfillkindg_none_p_kernel(tc, x_words, x_scales, wa, gt, w1, tab, offs, n1, n2, n3, n4, out):
+    nc = tc.nc
+    with ExitStack() as ctx:
+        lists = ctx.enter_context(tc.tile_pool(name="lists", bufs=1))
+        keep = ctx.enter_context(tc.tile_pool(name="keep", bufs=1))
+        psum = ctx.enter_context(tc.psum_pool(name="psum", bufs=1))
+
+        def load_list(src, name):
+            tile = lists.tile(list(src.shape), U16, name=name)
+            nc.sync.dma_start(tile[:], src)
+            return tile
+
+        tab_rows = tab.rearrange("(p t) c -> t p c", t=PACK)
+        out_rows = out.rearrange("(p t) c -> t p c", t=PACK)
+
+        def load_tab(t):
+            tile = keep.tile([P, 2 * J], F32, name=f"tab{t}")
+            nc.sync.dma_start(tile[:, 0:J], tab_rows[t])
+            return tile
+
+        scale_table = keep.tile([P, T], U8, name="scale_table", align_bytes=64)
+        nc.vector.memset(scale_table[:].bitcast(I32), 0)
+
+        offs_sb = load_list(offs, "offs_sb")
+        wa_rows = wa.rearrange("(p j) c -> p j c", j=PACK)
+        wa_raw = [keep.tile([P, PACK, HALF], F32, name=f"wa_raw{i}") for i in range(2)]
+        nc.sync.dma_start(wa_raw[0][:], wa_rows[:, :, 0:HALF])
+        for q in range(4):
+            nc.sync.dma_start(scale_table[32 * q : 32 * q + 4, :].bitcast(I32), x_scales[0, 4 * q : 4 * q + 4, :].bitcast(I32))
+        word_table = keep.tile([P, T], I32, name="word_table", align_bytes=64)
+        nc.sync.dma_start(word_table[:], x_words[0].rearrange("p c r -> p (c r)").bitcast(I32))
+        nc.sync.dma_start(wa_raw[1][:], wa_rows[:, :, HALF:H])
+        n3_sb = load_list(n3, "n3_sb")
+        tabs = [load_tab(0)]
+        n1_sb = load_list(n1, "n1_sb")
+        n2_sb = load_list(n2, "n2_sb")
+        gt_sb = keep.tile([P, PACK], F32, name="gt_sb")
+        nc.sync.dma_start(gt_sb[:], gt.rearrange("(p t) o -> p (t o)", t=PACK))
+        w1_raw = keep.tile([P, PACK, N], F32, name="w1_raw")
+        nc.sync.dma_start(w1_raw[:], w1.rearrange("(p j) c -> p j c", j=PACK))
+        n4_sb = load_list(n4, "n4_sb")
+        tabs.extend(load_tab(t) for t in range(1, PACK))
+
+        picked_scales = keep.tile([P, S], U8, name="picked_scales", align_bytes=64)
+        nc.vector.tensor_copy(picked_scales[:], scale_table[:].indirect(offs_sb[:]))
+        x_scale = keep.tile([P, S], U8, name="x_scale", align_bytes=64)
+        nc.vector.tensor_copy(x_scale[:].rearrange("p (t m) -> p t m", t=PACK), picked_scales[:].rearrange("p (m t) -> p t m", t=PACK))
+        picked_words = keep.tile([P, S], U32, name="picked_words", align_bytes=64)
+        nc.vector.tensor_copy(picked_words[:], word_table[:].bitcast(U32).indirect(offs_sb[:]))
+        x_code = keep.tile([P, S], I32, name="x_code", align_bytes=64)
+        nc.vector.tensor_copy(x_code[:].rearrange("p (t m) -> p m t", t=PACK), picked_words[:].bitcast(I32).rearrange("p (m t) -> p m t", t=PACK))
+
+        wa_code = keep.tile([P, H], U32, name="wa_code", align_bytes=64)
+        wa_scale = keep.tile([P, H], U8, name="wa_scale", align_bytes=64)
+        y_bank = [psum.tile([P, H], F32, name=f"y_bank{t}") for t in range(PACK)]
+        for i in range(2):
+            a, b = i * HALF, (i + 1) * HALF
+            grouped = keep.tile([P, HALF, PACK], BF16, name=f"wa_grouped{i}", align_bytes=64)
+            dst = grouped[:].rearrange("p (c i) j -> p c j i", i=4)
+            src = wa_raw[i][:].rearrange("p j (c i) -> p c j i", i=4)
+            if i == 0:
+                nc.scalar.copy(dst, src)
+            else:
+                nc.scalar.copy(dst[:, 0:32], src[:, 0:32])
+                nc.vector.tensor_copy(dst[:, 32:64], src[:, 32:64])
+            nc.vector.quantize_mx(wa_code[:, a:b].bitcast(FP8X4), wa_scale[:, a:b], grouped[:].rearrange("p c j -> p (c j)"))
+            for t in range(PACK):
+                cols = slice(P * t, P * (t + 1))
+                nc.tensor.matmul_mx(y_bank[t][:, a:b], lhsT=x_code[:, cols].bitcast(FP8X4), lhsT_scale=x_scale[:, cols],
+                                    rhs=wa_code[:, a:b].bitcast(FP8X4), rhs_scale=wa_scale[:, a:b], start=True, stop=True)
+
+        kind0 = keep.tile([P, H], F32, name="kind0")
+        nc.vector.tensor_copy(kind0[:], tabs[0][:].indirect(n3_sb[:]))
+
+        y = [keep.tile([P, H], F32, name=f"y{t}") for t in range(PACK)]
+        for t in range(PACK):
+            nc.scalar.copy(y[t][:], y_bank[t][:])
+
+        w1_grouped = keep.tile([P, PACK, P, PACK], BF16, name="w1_grouped", align_bytes=64)
+        nc.scalar.copy(w1_grouped[:].rearrange("p t m j -> p m j t"), w1_raw[:].rearrange("p j (m t) -> p m j t", t=PACK))
+        w1_code = keep.tile([P, N], U32, name="w1_code", align_bytes=64)
+        w1_scale = keep.tile([P, N], U8, name="w1_scale", align_bytes=64)
+
+        z_grouped = keep.tile([P, H, PACK], BF16, name="z_grouped", tag="after_z", align_bytes=64)
+        pa = [keep.tile([P, W], F32, name=f"pa{t}") for t in range(PACK)]
+        pb = [keep.tile([P, W], F32, name=f"pb{t}") for t in range(PACK)]
+        ra = [keep.tile([P, W], F32, name=f"ra{t}", tag=f"after_scatter{t}") for t in range(PACK)]
+
+        def fetch(t):
+            nc.vector.tensor_copy(pa[t][:], y[t][:].indirect(n1_sb[:]))
+            nc.vector.tensor_copy(pb[t][:], y[t][:].indirect(n2_sb[:]))
+
+        def larger(t):
+            nc.vector.tensor_tensor(ra[t][:], pa[t][:], pb[t][:], ALU.max)
+
+        def put(t):
+            nc.vector.tensor_copy(y[t][:].indirect(n1_sb[:]), ra[t][:])
+            nc.scalar.activation(z_grouped[:, :, t], y[t][:], COPY, scale=gt_sb[:, t : t + 1])
+
+        fetch(0)
+        for t in range(PACK):
+            if t + 1 < PACK:
+                fetch(t + 1)
+            larger(t)
+            if t == 1:
+                nc.vector.quantize_mx(w1_code[:].bitcast(FP8X4), w1_scale[:], w1_grouped[:].rearrange("p t m j -> p (t m j)"))
+            if t > 0:
+                put(t - 1)
+        put(PACK - 1)
+
+        kind = keep.tile([P, 2, H], F32, name="kind01", tag="after_scatter3")
+        for t in range(2):
+            nc.vector.tensor_copy(kind[:, t, :], tabs[1 + t][:].indirect(n3_sb[:]))
+        z_code = keep.tile([P, H], U32, name="z_code", align_bytes=64)
+        z_scale = keep.tile([P, H], U8, name="z_scale", align_bytes=64)
+        nc.vector.quantize_mx(z_code[:].bitcast(FP8X4), z_scale[:], z_grouped[:].rearrange("p c j -> p (c j)"))
+        kind_late = keep.tile([P, H], F32, name="kind3", tag="after_z", align_bytes=64)
+        nc.vector.tensor_copy(kind_late[:], tabs[3][:].indirect(n3_sb[:]))
+        kinds = [kind0[:], kind[:, 0, :], kind[:, 1, :], kind_late[:]]
+
+        h_bank = [psum.tile([P, H], F32, name=f"h_bank{t}") for t in range(PACK)]
+        for t in range(PACK):
+            cols = slice(P * t, P * (t + 1))
+            nc.tensor.matmul_mx(h_bank[t][:], lhsT=w1_code[:, cols].bitcast(FP8X4), lhsT_scale=w1_scale[:, cols],
+                                rhs=z_code[:].bitcast(FP8X4), rhs_scale=z_scale[:], start=True, stop=True)
+
+        half_h = [keep.tile([P, 2 * H], F32, name=f"half_h{t}") for t in range(PACK)]
+        prod = [keep.tile([P, H], F32, name=f"prod{t}") for t in range(PACK)]
+        res = [keep.tile([P, H], F32, name=f"res{t}") for t in range(PACK)]
+
+        def window(t):
+            nc.scalar.activation(half_h[t][:, 0:H], h_bank[t][:], COPY, scale=-0.5)
+
+        def product(t):
+            nc.vector.tensor_tensor(prod[t][:], h_bank[t][:], kinds[t], ALU.mult)
+
+        def finish(t):
+            pieces = ((0, H),) if t < PACK - 1 else ((0, H // 2), (H // 2, H))
+            for a, b in pieces:
+                nc.vector.tensor_tensor(res[t][:, a:b], half_h[t][:].indirect(n4_sb[:, a // 16 : b // 16]), prod[t][:, a:b], ALU.add)
+                nc.sync.dma_start(out_rows[t][:, a:b], res[t][:, a:b])
+
+        window(0)
+        product(1)
+        product(0)
+        window(2)
+        window(1)
+        window(3)
+        finish(0)
+        product(2)
+        finish(1)
+        product(3)
+        finish(2)
+        finish(3)

@@ -18,6 +18,7 @@ COPY = mybir.ActivationFunctionType.Copy
 P = 128
 PACK = 4
 HALF = H // 2
+WA_SCALAR_COLUMNS = (192, 96)
 
 
 def tile_picked_tokfillkindg_none_p_kernel(tc, x_words, x_scales, wa, gt, w1, tab, offs, n1, n2, n3, n4, out):
@@ -44,21 +45,23 @@ def tile_picked_tokfillkindg_none_p_kernel(tc, x_words, x_scales, wa, gt, w1, ta
         nc.vector.memset(scale_table[:].bitcast(I32), 0)
 
         offs_sb = load_list(offs, "offs_sb")
-        wa_rows = wa.rearrange("(p j) c -> p j c", j=PACK)
-        wa_raw = [keep.tile([P, PACK, HALF], F32, name=f"wa_raw{i}") for i in range(2)]
-        nc.sync.dma_start(wa_raw[0][:], wa_rows[:, :, 0:HALF])
+        word_table = keep.tile([P, T], I32, name="word_table", align_bytes=64)
+        x_rows = x_words[0].rearrange("p c r -> p (c r)").bitcast(I32)
+        nc.sync.dma_start(word_table[:, 0 : T // 4], x_rows[:, 0 : T // 4])
         for q in range(4):
             nc.sync.dma_start(scale_table[32 * q : 32 * q + 4, :].bitcast(I32), x_scales[0, 4 * q : 4 * q + 4, :].bitcast(I32))
-        word_table = keep.tile([P, T], I32, name="word_table", align_bytes=64)
-        nc.sync.dma_start(word_table[:], x_words[0].rearrange("p c r -> p (c r)").bitcast(I32))
-        nc.sync.dma_start(wa_raw[1][:], wa_rows[:, :, HALF:H])
+        nc.sync.dma_start(word_table[:, T // 4 : T], x_rows[:, T // 4 : T])
+        wa_rows = wa.rearrange("(p j) c -> p j c", j=PACK)
+        wa_raw = [keep.tile([P, PACK, HALF], F32, name=f"wa_raw{i}") for i in range(2)]
+        for i in range(2):
+            nc.sync.dma_start(wa_raw[i][:], wa_rows[:, :, i * HALF : (i + 1) * HALF])
         n3_sb = load_list(n3, "n3_sb")
         tabs = [load_tab(0)]
         n1_sb = load_list(n1, "n1_sb")
         n2_sb = load_list(n2, "n2_sb")
         gt_sb = keep.tile([P, PACK], F32, name="gt_sb")
         nc.sync.dma_start(gt_sb[:], gt.rearrange("(p t) o -> p (t o)", t=PACK))
-        w1_raw = keep.tile([P, PACK, N], F32, name="w1_raw")
+        w1_raw = keep.tile([P, PACK, N], F32, name="w1_raw", tag="staging", align_bytes=64)
         nc.sync.dma_start(w1_raw[:], w1.rearrange("(p j) c -> p j c", j=PACK))
         n4_sb = load_list(n4, "n4_sb")
         tabs.extend(load_tab(t) for t in range(1, PACK))
@@ -74,24 +77,28 @@ def tile_picked_tokfillkindg_none_p_kernel(tc, x_words, x_scales, wa, gt, w1, ta
 
         wa_code = keep.tile([P, H], U32, name="wa_code", align_bytes=64)
         wa_scale = keep.tile([P, H], U8, name="wa_scale", align_bytes=64)
-        y_bank = [psum.tile([P, H], F32, name=f"y_bank{t}") for t in range(PACK)]
+        y_bank = [psum.tile([P, H], F32, name=f"y_bank{t}", tag=f"bank{t}") for t in range(PACK)]
+
+        def project(t, a, b):
+            cols = slice(P * t, P * (t + 1))
+            nc.tensor.matmul_mx(y_bank[t][:, a:b], lhsT=x_code[:, cols].bitcast(FP8X4), lhsT_scale=x_scale[:, cols],
+                                rhs=wa_code[:, a:b].bitcast(FP8X4), rhs_scale=wa_scale[:, a:b], start=True, stop=True)
+
         for i in range(2):
             a, b = i * HALF, (i + 1) * HALF
             grouped = keep.tile([P, HALF, PACK], BF16, name=f"wa_grouped{i}", align_bytes=64)
             dst = grouped[:].rearrange("p (c i) j -> p c j i", i=4)
             src = wa_raw[i][:].rearrange("p j (c i) -> p c j i", i=4)
-            if i == 0:
-                nc.scalar.copy(dst, src)
-            else:
-                nc.scalar.copy(dst[:, 0:32], src[:, 0:32])
-                nc.vector.tensor_copy(dst[:, 32:64], src[:, 32:64])
+            cut = WA_SCALAR_COLUMNS[i] // 4
+            nc.scalar.copy(dst[:, :cut], src[:, :cut])
+            nc.vector.tensor_copy(dst[:, cut:], src[:, cut:])
             nc.vector.quantize_mx(wa_code[:, a:b].bitcast(FP8X4), wa_scale[:, a:b], grouped[:].rearrange("p c j -> p (c j)"))
-            for t in range(PACK):
-                cols = slice(P * t, P * (t + 1))
-                nc.tensor.matmul_mx(y_bank[t][:, a:b], lhsT=x_code[:, cols].bitcast(FP8X4), lhsT_scale=x_scale[:, cols],
-                                    rhs=wa_code[:, a:b].bitcast(FP8X4), rhs_scale=wa_scale[:, a:b], start=True, stop=True)
+            for t in range(2):
+                project(t, a, b)
+        for t in range(2, PACK):
+            project(t, 0, H)
 
-        kind0 = keep.tile([P, H], F32, name="kind0")
+        kind0 = keep.tile([P, H], F32, name="kind0", tag="wa_grouped1", align_bytes=64)
         nc.vector.tensor_copy(kind0[:], tabs[0][:].indirect(n3_sb[:]))
 
         y = [keep.tile([P, H], F32, name=f"y{t}") for t in range(PACK)]
@@ -100,61 +107,76 @@ def tile_picked_tokfillkindg_none_p_kernel(tc, x_words, x_scales, wa, gt, w1, ta
 
         w1_grouped = keep.tile([P, PACK, P, PACK], BF16, name="w1_grouped", align_bytes=64)
         nc.scalar.copy(w1_grouped[:].rearrange("p t m j -> p m j t"), w1_raw[:].rearrange("p j (m t) -> p m j t", t=PACK))
-        w1_code = keep.tile([P, N], U32, name="w1_code", align_bytes=64)
         w1_scale = keep.tile([P, N], U8, name="w1_scale", align_bytes=64)
 
-        z_grouped = keep.tile([P, H, PACK], BF16, name="z_grouped", tag="after_z", align_bytes=64)
-        pa = [keep.tile([P, W], F32, name=f"pa{t}") for t in range(PACK)]
-        pb = [keep.tile([P, W], F32, name=f"pb{t}") for t in range(PACK)]
-        ra = [keep.tile([P, W], F32, name=f"ra{t}", tag=f"after_scatter{t}") for t in range(PACK)]
+        z_grouped = keep.tile([P, H, PACK], BF16, name="z_grouped", tag="staging", align_bytes=64)
+        pa = [keep.tile([P, 2, W], F32, name=f"pa{u}") for u in range(2)]
+        pb = [keep.tile([P, 2, W], F32, name=f"pb{u}") for u in range(2)]
+        ra = [keep.tile([P, 2, W], F32, name=f"ra{u}", tag=f"after_scatter{u}", align_bytes=64) for u in range(2)]
 
         def fetch(t):
-            nc.vector.tensor_copy(pa[t][:], y[t][:].indirect(n1_sb[:]))
-            nc.vector.tensor_copy(pb[t][:], y[t][:].indirect(n2_sb[:]))
+            nc.vector.tensor_copy(pa[t // 2][:, t % 2, :], y[t][:].indirect(n1_sb[:]))
+            nc.vector.tensor_copy(pb[t // 2][:, t % 2, :], y[t][:].indirect(n2_sb[:]))
 
-        def larger(t):
-            nc.vector.tensor_tensor(ra[t][:], pa[t][:], pb[t][:], ALU.max)
+        def larger(u):
+            nc.vector.tensor_tensor(ra[u][:], pa[u][:], pb[u][:], ALU.max)
 
         def put(t):
-            nc.vector.tensor_copy(y[t][:].indirect(n1_sb[:]), ra[t][:])
-            nc.scalar.activation(z_grouped[:, :, t], y[t][:], COPY, scale=gt_sb[:, t : t + 1])
+            nc.vector.tensor_copy(y[t][:].indirect(n1_sb[:]), ra[t // 2][:, t % 2, :])
+            pieces = ((0, H),) if t < PACK - 1 else ((0, HALF), (HALF, H))
+            for a, b in pieces:
+                nc.scalar.activation(z_grouped[:, a:b, t], y[t][:, a:b], COPY, scale=gt_sb[:, t : t + 1])
 
         fetch(0)
-        for t in range(PACK):
-            if t + 1 < PACK:
-                fetch(t + 1)
-            larger(t)
-            if t == 1:
-                nc.vector.quantize_mx(w1_code[:].bitcast(FP8X4), w1_scale[:], w1_grouped[:].rearrange("p t m j -> p (t m j)"))
-            if t > 0:
-                put(t - 1)
-        put(PACK - 1)
+        fetch(1)
+        larger(0)
+        fetch(2)
+        put(0)
+        fetch(3)
+        larger(1)
+        put(1)
+        put(2)
+        put(3)
 
-        kind = keep.tile([P, 2, H], F32, name="kind01", tag="after_scatter3")
-        for t in range(2):
-            nc.vector.tensor_copy(kind[:, t, :], tabs[1 + t][:].indirect(n3_sb[:]))
+        w1_code = keep.tile([P, N], U32, name="w1_code", tag="after_scatter1", align_bytes=64)
+        nc.vector.quantize_mx(w1_code[:].bitcast(FP8X4), w1_scale[:], w1_grouped[:].rearrange("p t m j -> p (t m j)"))
         z_code = keep.tile([P, H], U32, name="z_code", align_bytes=64)
         z_scale = keep.tile([P, H], U8, name="z_scale", align_bytes=64)
-        nc.vector.quantize_mx(z_code[:].bitcast(FP8X4), z_scale[:], z_grouped[:].rearrange("p c j -> p (c j)"))
-        kind_late = keep.tile([P, H], F32, name="kind3", tag="after_z", align_bytes=64)
-        nc.vector.tensor_copy(kind_late[:], tabs[3][:].indirect(n3_sb[:]))
-        kinds = [kind0[:], kind[:, 0, :], kind[:, 1, :], kind_late[:]]
 
-        h_bank = [psum.tile([P, H], F32, name=f"h_bank{t}") for t in range(PACK)]
-        for t in range(PACK):
+        def quantize_z(a, b):
+            nc.vector.quantize_mx(z_code[:, a:b].bitcast(FP8X4), z_scale[:, a:b], z_grouped[:, a:b, :].rearrange("p c j -> p (c j)"))
+
+        def mix(t, a, b, bank):
             cols = slice(P * t, P * (t + 1))
-            nc.tensor.matmul_mx(h_bank[t][:], lhsT=w1_code[:, cols].bitcast(FP8X4), lhsT_scale=w1_scale[:, cols],
-                                rhs=z_code[:].bitcast(FP8X4), rhs_scale=z_scale[:], start=True, stop=True)
+            nc.tensor.matmul_mx(bank, lhsT=w1_code[:, cols].bitcast(FP8X4), lhsT_scale=w1_scale[:, cols],
+                                rhs=z_code[:, a:b].bitcast(FP8X4), rhs_scale=z_scale[:, a:b], start=True, stop=True)
 
         half_h = [keep.tile([P, 2 * H], F32, name=f"half_h{t}") for t in range(PACK)]
+        first = [psum.tile([P, HALF], F32, name=f"h0_bank{i}") for i in range(2)]
+        for i in range(2):
+            a, b = i * HALF, (i + 1) * HALF
+            quantize_z(a, b)
+            mix(0, a, b, first[i][:])
+            nc.scalar.activation(half_h[0][:, a:b], first[i][:], COPY, scale=-0.5)
+        kind1 = keep.tile([P, H], F32, name="kind1", tag="staging", align_bytes=64)
+        nc.vector.tensor_copy(kind1[:], tabs[1][:].indirect(n3_sb[:]))
+        kinds = [kind0, kind1]
+        h_bank = [None] + [psum.tile([P, H], F32, name=f"h_bank{t}", tag=f"bank{t}") for t in range(1, PACK)]
+        h = [None, None] + [keep.tile([P, H], F32, name=f"h{t}") for t in range(2, PACK)]
+        for t in range(1, PACK):
+            mix(t, 0, H, h_bank[t][:])
+            if t >= 2:
+                nc.scalar.copy(h[t][:], h_bank[t][:])
+            nc.scalar.activation(half_h[t][:, 0:H], h_bank[t][:], COPY, scale=-0.5)
+
         prod = [keep.tile([P, H], F32, name=f"prod{t}") for t in range(PACK)]
         res = [keep.tile([P, H], F32, name=f"res{t}") for t in range(PACK)]
 
-        def window(t):
-            nc.scalar.activation(half_h[t][:, 0:H], h_bank[t][:], COPY, scale=-0.5)
-
         def product(t):
-            nc.vector.tensor_tensor(prod[t][:], h_bank[t][:], kinds[t], ALU.mult)
+            if t < 2:
+                nc.vector.scalar_tensor_tensor(prod[t][:], half_h[t][:, 0:H], -2.0, kinds[t][:], ALU.mult, ALU.mult)
+            else:
+                nc.vector.tensor_tensor(prod[t][:], tabs[t][:].indirect(n3_sb[:]), h[t][:], ALU.mult)
 
         def finish(t):
             pieces = ((0, H),) if t < PACK - 1 else ((0, H // 2), (H // 2, H))
@@ -162,15 +184,8 @@ def tile_picked_tokfillkindg_none_p_kernel(tc, x_words, x_scales, wa, gt, w1, ta
                 nc.vector.tensor_tensor(res[t][:, a:b], half_h[t][:].indirect(n4_sb[:, a // 16 : b // 16]), prod[t][:, a:b], ALU.add)
                 nc.sync.dma_start(out_rows[t][:, a:b], res[t][:, a:b])
 
-        window(0)
-        product(1)
         product(0)
-        window(2)
-        window(1)
-        window(3)
-        finish(0)
-        product(2)
-        finish(1)
-        product(3)
-        finish(2)
-        finish(3)
+        for t in range(PACK):
+            if t + 1 < PACK:
+                product(t + 1)
+            finish(t)

@@ -14,6 +14,7 @@ U8 = mybir.dt.uint8
 FP8X4 = mybir.dt.float8_e4m3fn_x4
 ALU = mybir.AluOpType
 COPY = mybir.ActivationFunctionType.Copy
+RELU = mybir.ActivationFunctionType.Relu
 
 P = 128
 PACK = 4
@@ -61,7 +62,7 @@ def tile_picked_tokfillkindg_none_p_kernel(tc, x_words, x_scales, wa, gt, w1, ta
         n2_sb = load_list(n2, "n2_sb")
         gt_sb = keep.tile([P, PACK], F32, name="gt_sb")
         nc.sync.dma_start(gt_sb[:], gt.rearrange("(p t) o -> p (t o)", t=PACK))
-        w1_raw = keep.tile([P, PACK, N], F32, name="w1_raw", tag="staging", align_bytes=64)
+        w1_raw = keep.tile([P, PACK, N], F32, name="w1_raw", align_bytes=64)
         nc.sync.dma_start(w1_raw[:], w1.rearrange("(p j) c -> p j c", j=PACK))
         n4_sb = load_list(n4, "n4_sb")
         tabs.extend(load_tab(t) for t in range(1, PACK))
@@ -77,12 +78,14 @@ def tile_picked_tokfillkindg_none_p_kernel(tc, x_words, x_scales, wa, gt, w1, ta
 
         wa_code = keep.tile([P, H], U32, name="wa_code", align_bytes=64)
         wa_scale = keep.tile([P, H], U8, name="wa_scale", align_bytes=64)
-        y_bank = [psum.tile([P, H], F32, name=f"y_bank{t}", tag=f"bank{t}") for t in range(PACK)]
+        y = [keep.tile([P, H], F32, name=f"y{t}") for t in range(PACK)]
 
         def project(t, a, b):
             cols = slice(P * t, P * (t + 1))
-            nc.tensor.matmul_mx(y_bank[t][:, a:b], lhsT=x_code[:, cols].bitcast(FP8X4), lhsT_scale=x_scale[:, cols],
+            bank = psum.tile([P, b - a], F32, name=f"y_bank{t}_{a}")
+            nc.tensor.matmul_mx(bank[:], lhsT=x_code[:, cols].bitcast(FP8X4), lhsT_scale=x_scale[:, cols],
                                 rhs=wa_code[:, a:b].bitcast(FP8X4), rhs_scale=wa_scale[:, a:b], start=True, stop=True)
+            return bank
 
         for i in range(2):
             a, b = i * HALF, (i + 1) * HALF
@@ -94,52 +97,41 @@ def tile_picked_tokfillkindg_none_p_kernel(tc, x_words, x_scales, wa, gt, w1, ta
             nc.vector.tensor_copy(dst[:, cut:], src[:, cut:])
             nc.vector.quantize_mx(wa_code[:, a:b].bitcast(FP8X4), wa_scale[:, a:b], grouped[:].rearrange("p c j -> p (c j)"))
             for t in range(2):
-                project(t, a, b)
-        for t in range(2, PACK):
-            project(t, 0, H)
+                nc.scalar.copy(y[t][:, a:b], project(t, a, b)[:])
+        y_bank = {t: project(t, 0, H) for t in range(2, PACK)}
 
         kind0 = keep.tile([P, H], F32, name="kind0", tag="wa_grouped1", align_bytes=64)
         nc.vector.tensor_copy(kind0[:], tabs[0][:].indirect(n3_sb[:]))
 
-        y = [keep.tile([P, H], F32, name=f"y{t}") for t in range(PACK)]
-        for t in range(PACK):
-            nc.scalar.copy(y[t][:], y_bank[t][:])
+        nc.scalar.copy(y[2][:, : H - 64], y_bank[2][:, : H - 64])
+        nc.scalar.copy(y[3][:], y_bank[3][:])
+        nc.scalar.copy(y[2][:, H - 64 :], y_bank[2][:, H - 64 :])
 
         w1_grouped = keep.tile([P, PACK, P, PACK], BF16, name="w1_grouped", align_bytes=64)
         nc.scalar.copy(w1_grouped[:].rearrange("p t m j -> p m j t"), w1_raw[:].rearrange("p j (m t) -> p m j t", t=PACK))
         w1_scale = keep.tile([P, N], U8, name="w1_scale", align_bytes=64)
 
-        z_grouped = keep.tile([P, H, PACK], BF16, name="z_grouped", tag="staging", align_bytes=64)
-        pa = [keep.tile([P, 2, W], F32, name=f"pa{u}") for u in range(2)]
-        pb = [keep.tile([P, 2, W], F32, name=f"pb{u}") for u in range(2)]
-        ra = [keep.tile([P, 2, W], F32, name=f"ra{u}", tag=f"after_scatter{u}", align_bytes=64) for u in range(2)]
-
-        def fetch(t):
-            nc.vector.tensor_copy(pa[t // 2][:, t % 2, :], y[t][:].indirect(n1_sb[:]))
-            nc.vector.tensor_copy(pb[t // 2][:, t % 2, :], y[t][:].indirect(n2_sb[:]))
-
-        def larger(u):
-            nc.vector.tensor_tensor(ra[u][:], pa[u][:], pb[u][:], ALU.max)
-
-        def put(t):
-            nc.vector.tensor_copy(y[t][:].indirect(n1_sb[:]), ra[t // 2][:, t % 2, :])
+        z_grouped = keep.tile([P, H, PACK], BF16, name="z_grouped", align_bytes=64)
+        pa = [keep.tile([P, W], F32, name=f"pa{t}") for t in range(PACK)]
+        excess = [keep.tile([P, 2, W], F32, name="excess0", tag="wa_code", align_bytes=64), keep.tile([P, 2, W], F32, name="excess1")]
+        rise = keep.tile([P, PACK, W], F32, name="rise", tag="w1_raw", align_bytes=64)
+        for pair in ((0, 1), (3, 2)):
+            for t in pair:
+                nc.vector.tensor_copy(pa[t][:], y[t][:].indirect(n1_sb[:]))
+            for t in pair:
+                nc.vector.tensor_tensor(excess[t // 2][:, t % 2, :], y[t][:].indirect(n2_sb[:]), pa[t][:], ALU.subtract)
+        for t in range(PACK):
+            nc.scalar.activation(rise[:, t, :], excess[t // 2][:, t % 2, :], RELU)
+        for t in range(PACK):
+            nc.vector.tensor_tensor(y[t][:].indirect(n1_sb[:]), pa[t][:], rise[:, t, :], ALU.add)
             pieces = ((0, H),) if t < PACK - 1 else ((0, HALF), (HALF, H))
             for a, b in pieces:
                 nc.scalar.activation(z_grouped[:, a:b, t], y[t][:, a:b], COPY, scale=gt_sb[:, t : t + 1])
 
-        fetch(0)
-        fetch(1)
-        larger(0)
-        fetch(2)
-        put(0)
-        fetch(3)
-        larger(1)
-        put(1)
-        put(2)
-        put(3)
-
-        w1_code = keep.tile([P, N], U32, name="w1_code", tag="after_scatter1", align_bytes=64)
+        w1_code = keep.tile([P, N], U32, name="w1_code", tag="w1_raw", align_bytes=64)
         nc.vector.quantize_mx(w1_code[:].bitcast(FP8X4), w1_scale[:], w1_grouped[:].rearrange("p t m j -> p (t m j)"))
+        kind2 = keep.tile([P, H], F32, name="kind2", tag="w1_grouped", align_bytes=64)
+        nc.vector.tensor_copy(kind2[:], tabs[1][:].indirect(n3_sb[:]))
         z_code = keep.tile([P, H], U32, name="z_code", align_bytes=64)
         z_scale = keep.tile([P, H], U8, name="z_scale", align_bytes=64)
 
@@ -158,14 +150,14 @@ def tile_picked_tokfillkindg_none_p_kernel(tc, x_words, x_scales, wa, gt, w1, ta
             quantize_z(a, b)
             mix(0, a, b, first[i][:])
             nc.scalar.activation(half_h[0][:, a:b], first[i][:], COPY, scale=-0.5)
-        kind1 = keep.tile([P, H], F32, name="kind1", tag="staging", align_bytes=64)
-        nc.vector.tensor_copy(kind1[:], tabs[1][:].indirect(n3_sb[:]))
-        kinds = [kind0, kind1]
-        h_bank = [None] + [psum.tile([P, H], F32, name=f"h_bank{t}", tag=f"bank{t}") for t in range(1, PACK)]
-        h = [None, None] + [keep.tile([P, H], F32, name=f"h{t}") for t in range(2, PACK)]
+        kind1 = keep.tile([P, H], F32, name="kind1", tag="z_grouped", align_bytes=64)
+        nc.vector.tensor_copy(kind1[:], tabs[2][:].indirect(n3_sb[:]))
+        kinds = [kind0, kind2, kind1]
+        h_bank = [None] + [psum.tile([P, H], F32, name=f"h_bank{t}", tag=f"y_bank{t}_0") for t in range(1, PACK)]
+        h = [None, None, None] + [keep.tile([P, H], F32, name=f"h{t}") for t in range(3, PACK)]
         for t in range(1, PACK):
             mix(t, 0, H, h_bank[t][:])
-            if t >= 2:
+            if t >= 3:
                 nc.scalar.copy(h[t][:], h_bank[t][:])
             nc.scalar.activation(half_h[t][:, 0:H], h_bank[t][:], COPY, scale=-0.5)
 
@@ -173,7 +165,7 @@ def tile_picked_tokfillkindg_none_p_kernel(tc, x_words, x_scales, wa, gt, w1, ta
         res = [keep.tile([P, H], F32, name=f"res{t}") for t in range(PACK)]
 
         def product(t):
-            if t < 2:
+            if t < 3:
                 nc.vector.scalar_tensor_tensor(prod[t][:], half_h[t][:, 0:H], -2.0, kinds[t][:], ALU.mult, ALU.mult)
             else:
                 nc.vector.tensor_tensor(prod[t][:], tabs[t][:].indirect(n3_sb[:]), h[t][:], ALU.mult)

from contextlib import ExitStack

import concourse.mybir as mybir

K, T, S, N, H, W, J = 512, 2048, 512, 512, 512, 256, 512
FLOPS = 2 * K * S * H + 2 * S * N * H

F32 = mybir.dt.float32
BF16 = mybir.dt.bfloat16
I32 = mybir.dt.int32
U32 = mybir.dt.uint32
U16 = mybir.dt.uint16
U8 = mybir.dt.uint8
FP8X4 = mybir.dt.float8_e4m3fn_x4
ALU = mybir.AluOpType
COPY = mybir.ActivationFunctionType.Copy
RELU = mybir.ActivationFunctionType.Relu

P = 128
PACK = 4
HALF = H // 2
WA_SCALAR_COLUMNS = (192, 96)


def tile_picked_tokfillkindg_none_p_kernel(tc, x_words, x_scales, wa, gt, w1, tab, offs, n1, n2, n3, n4, out):
    nc = tc.nc
    with ExitStack() as ctx:
        lists = ctx.enter_context(tc.tile_pool(name="lists", bufs=1))
        keep = ctx.enter_context(tc.tile_pool(name="keep", bufs=1))
        psum = ctx.enter_context(tc.psum_pool(name="psum", bufs=1))

        def load_list(src, name):
            tile = lists.tile(list(src.shape), U16, name=name)
            nc.sync.dma_start(tile[:], src)
            return tile

        tab_rows = tab.rearrange("(p t) c -> t p c", t=PACK)
        out_rows = out.rearrange("(p t) c -> t p c", t=PACK)

        def load_tab(t):
            tile = keep.tile([P, 2 * J], F32, name=f"tab{t}")
            nc.sync.dma_start(tile[:, 0:J], tab_rows[t])
            return tile

        scale_table = keep.tile([P, T], U8, name="scale_table", align_bytes=64)
        nc.vector.memset(scale_table[:].bitcast(I32), 0)

        offs_sb = load_list(offs, "offs_sb")
        word_table = keep.tile([P, T], I32, name="word_table", align_bytes=64)
        x_rows = x_words[0].rearrange("p c r -> p (c r)").bitcast(I32)
        nc.sync.dma_start(word_table[:, 0 : T // 4], x_rows[:, 0 : T // 4])
        for q in range(4):
            nc.sync.dma_start(scale_table[32 * q : 32 * q + 4, :].bitcast(I32), x_scales[0, 4 * q : 4 * q + 4, :].bitcast(I32))
        nc.sync.dma_start(word_table[:, T // 4 : T], x_rows[:, T // 4 : T])
        wa_rows = wa.rearrange("(p j) c -> p j c", j=PACK)
        wa_raw = [keep.tile([P, PACK, HALF], F32, name=f"wa_raw{i}") for i in range(2)]
        for i in range(2):
            nc.sync.dma_start(wa_raw[i][:], wa_rows[:, :, i * HALF : (i + 1) * HALF])
        n3_sb = load_list(n3, "n3_sb")
        tabs = [load_tab(0)]
        n1_sb = load_list(n1, "n1_sb")
        n2_sb = load_list(n2, "n2_sb")
        gt_sb = keep.tile([P, PACK], F32, name="gt_sb")
        nc.sync.dma_start(gt_sb[:], gt.rearrange("(p t) o -> p (t o)", t=PACK))
        w1_raw = keep.tile([P, PACK, N], F32, name="w1_raw", align_bytes=64)
        nc.sync.dma_start(w1_raw[:], w1.rearrange("(p j) c -> p j c", j=PACK))
        n4_sb = load_list(n4, "n4_sb")
        tabs.extend(load_tab(t) for t in range(1, PACK))

        picked_scales = keep.tile([P, S], U8, name="picked_scales", align_bytes=64)
        nc.vector.tensor_copy(picked_scales[:], scale_table[:].indirect(offs_sb[:]))
        x_scale = keep.tile([P, S], U8, name="x_scale", align_bytes=64)
        nc.vector.tensor_copy(x_scale[:].rearrange("p (t m) -> p t m", t=PACK), picked_scales[:].rearrange("p (m t) -> p t m", t=PACK))
        picked_words = keep.tile([P, S], U32, name="picked_words", align_bytes=64)
        nc.vector.tensor_copy(picked_words[:], word_table[:].bitcast(U32).indirect(offs_sb[:]))
        x_code = keep.tile([P, S], I32, name="x_code", align_bytes=64)
        nc.vector.tensor_copy(x_code[:].rearrange("p (t m) -> p m t", t=PACK), picked_words[:].bitcast(I32).rearrange("p (m t) -> p m t", t=PACK))

        wa_code = keep.tile([P, H], U32, name="wa_code", align_bytes=64)
        wa_scale = keep.tile([P, H], U8, name="wa_scale", align_bytes=64)
        y = [keep.tile([P, H], F32, name=f"y{t}") for t in range(PACK)]

        def project(t, a, b):
            cols = slice(P * t, P * (t + 1))
            bank = psum.tile([P, b - a], F32, name=f"y_bank{t}_{a}")
            nc.tensor.matmul_mx(bank[:], lhsT=x_code[:, cols].bitcast(FP8X4), lhsT_scale=x_scale[:, cols],
                                rhs=wa_code[:, a:b].bitcast(FP8X4), rhs_scale=wa_scale[:, a:b], start=True, stop=True)
            return bank

        for i in range(2):
            a, b = i * HALF, (i + 1) * HALF
            grouped = keep.tile([P, HALF, PACK], BF16, name=f"wa_grouped{i}", align_bytes=64)
            dst = grouped[:].rearrange("p (c i) j -> p c j i", i=4)
            src = wa_raw[i][:].rearrange("p j (c i) -> p c j i", i=4)
            cut = WA_SCALAR_COLUMNS[i] // 4
            nc.scalar.copy(dst[:, :cut], src[:, :cut])
            nc.vector.tensor_copy(dst[:, cut:], src[:, cut:])
            nc.vector.quantize_mx(wa_code[:, a:b].bitcast(FP8X4), wa_scale[:, a:b], grouped[:].rearrange("p c j -> p (c j)"))
            for t in range(2):
                nc.scalar.copy(y[t][:, a:b], project(t, a, b)[:])
        y_bank = {t: project(t, 0, H) for t in range(2, PACK)}

        kind0 = keep.tile([P, H], F32, name="kind0", tag="wa_grouped1", align_bytes=64)
        nc.vector.tensor_copy(kind0[:], tabs[0][:].indirect(n3_sb[:]))

        nc.scalar.copy(y[2][:, : H - 64], y_bank[2][:, : H - 64])
        nc.scalar.copy(y[3][:], y_bank[3][:])
        nc.scalar.copy(y[2][:, H - 64 :], y_bank[2][:, H - 64 :])

        w1_grouped = keep.tile([P, PACK, P, PACK], BF16, name="w1_grouped", align_bytes=64)
        nc.scalar.copy(w1_grouped[:].rearrange("p t m j -> p m j t"), w1_raw[:].rearrange("p j (m t) -> p m j t", t=PACK))
        w1_scale = keep.tile([P, N], U8, name="w1_scale", align_bytes=64)

        z_grouped = keep.tile([P, H, PACK], BF16, name="z_grouped", align_bytes=64)
        pa = [keep.tile([P, W], F32, name=f"pa{t}") for t in range(PACK)]
        excess = [keep.tile([P, 2, W], F32, name="excess0", tag="wa_code", align_bytes=64), keep.tile([P, 2, W], F32, name="excess1")]
        rise = keep.tile([P, PACK, W], F32, name="rise", tag="w1_raw", align_bytes=64)
        for pair in ((0, 1), (3, 2)):
            for t in pair:
                nc.vector.tensor_copy(pa[t][:], y[t][:].indirect(n1_sb[:]))
            for t in pair:
                nc.vector.tensor_tensor(excess[t // 2][:, t % 2, :], y[t][:].indirect(n2_sb[:]), pa[t][:], ALU.subtract)
        for t in range(PACK):
            nc.scalar.activation(rise[:, t, :], excess[t // 2][:, t % 2, :], RELU)
        for t in range(PACK):
            nc.vector.tensor_tensor(y[t][:].indirect(n1_sb[:]), pa[t][:], rise[:, t, :], ALU.add)
            pieces = ((0, H),) if t < PACK - 1 else ((0, HALF), (HALF, H))
            for a, b in pieces:
                nc.scalar.activation(z_grouped[:, a:b, t], y[t][:, a:b], COPY, scale=gt_sb[:, t : t + 1])

        w1_code = keep.tile([P, N], U32, name="w1_code", tag="w1_raw", align_bytes=64)
        nc.vector.quantize_mx(w1_code[:].bitcast(FP8X4), w1_scale[:], w1_grouped[:].rearrange("p t m j -> p (t m j)"))
        kind2 = keep.tile([P, H], F32, name="kind2", tag="w1_grouped", align_bytes=64)
        nc.vector.tensor_copy(kind2[:], tabs[1][:].indirect(n3_sb[:]))
        z_code = keep.tile([P, H], U32, name="z_code", align_bytes=64)
        z_scale = keep.tile([P, H], U8, name="z_scale", align_bytes=64)

        def quantize_z(a, b):
            nc.vector.quantize_mx(z_code[:, a:b].bitcast(FP8X4), z_scale[:, a:b], z_grouped[:, a:b, :].rearrange("p c j -> p (c j)"))

        def mix(t, a, b, bank):
            cols = slice(P * t, P * (t + 1))
            nc.tensor.matmul_mx(bank, lhsT=w1_code[:, cols].bitcast(FP8X4), lhsT_scale=w1_scale[:, cols],
                                rhs=z_code[:, a:b].bitcast(FP8X4), rhs_scale=z_scale[:, a:b], start=True, stop=True)

        half_h = [keep.tile([P, 2 * H], F32, name=f"half_h{t}") for t in range(PACK)]
        first = [psum.tile([P, HALF], F32, name=f"h0_bank{i}") for i in range(2)]
        for i in range(2):
            a, b = i * HALF, (i + 1) * HALF
            quantize_z(a, b)
            mix(0, a, b, first[i][:])
            nc.scalar.activation(half_h[0][:, a:b], first[i][:], COPY, scale=-0.5)
        kind1 = keep.tile([P, H], F32, name="kind1", tag="z_grouped", align_bytes=64)
        nc.vector.tensor_copy(kind1[:], tabs[2][:].indirect(n3_sb[:]))
        kinds = [kind0, kind2, kind1]
        h_bank = [None] + [psum.tile([P, H], F32, name=f"h_bank{t}", tag=f"y_bank{t}_0") for t in range(1, PACK)]
        h = [None, None, None] + [keep.tile([P, H], F32, name=f"h{t}") for t in range(3, PACK)]
        for t in range(1, PACK):
            mix(t, 0, H, h_bank[t][:])
            if t >= 3:
                nc.scalar.copy(h[t][:], h_bank[t][:])
            nc.scalar.activation(half_h[t][:, 0:H], h_bank[t][:], COPY, scale=-0.5)

        prod = [keep.tile([P, H], F32, name=f"prod{t}") for t in range(PACK)]
        res = [keep.tile([P, H], F32, name=f"res{t}") for t in range(PACK)]

        def product(t):
            if t < 3:
                nc.vector.scalar_tensor_tensor(prod[t][:], half_h[t][:, 0:H], -2.0, kinds[t][:], ALU.mult, ALU.mult)
            else:
                nc.vector.tensor_tensor(prod[t][:], tabs[t][:].indirect(n3_sb[:]), h[t][:], ALU.mult)

        def finish(t):
            pieces = ((0, H),) if t < PACK - 1 else ((0, H // 2), (H // 2, H))
            for a, b in pieces:
                nc.vector.tensor_tensor(res[t][:, a:b], half_h[t][:].indirect(n4_sb[:, a // 16 : b // 16]), prod[t][:, a:b], ALU.add)
                nc.sync.dma_start(out_rows[t][:, a:b], res[t][:, a:b])

        product(0)
        for t in range(PACK):
            if t + 1 < PACK:
                product(t + 1)
            finish(t)
